import numpy as np
import ml_dtypes

BF16 = ml_dtypes.bfloat16


def bf(x):
    return np.asarray(x, np.float32).astype(BF16)


def f32(x):
    return np.asarray(x, np.float32)


def f64(x):
    return np.asarray(x).astype(np.float64)


def striped(idx):
    return np.tile(idx.reshape(-1, 16).T, (8, 1))


S, A, K, M, N, E, Q = 512, 128, 128, 512, 384, 4, 96


def gelu_tanh(v):
    return 0.5 * v * (1.0 + np.tanh(np.sqrt(2.0 / np.pi) * (v + 0.044715 * v**3)))


def setup_inputs():
    return {"x": bf(np.random.standard_normal((A, S))), "wd": bf(np.random.standard_normal((A, M)) / np.sqrt(A)), "y": bf(np.random.standard_normal((K, N))), "w": bf(np.random.standard_normal((E, K, M)) / np.sqrt(K)), "b": f32(0.5 * np.random.standard_normal((M, 1))), "offs": striped(np.random.permutation(S)[:N])}


def reference(x, wd, y, w, b, offs):
    idx = offs[:16].T.reshape(-1)
    z = f64(wd).T @ f64(x)
    for e in range(E):
        z[:, idx[e * Q : (e + 1) * Q]] += f64(w)[e].T @ f64(y)[:, e * Q : (e + 1) * Q]
    return gelu_tanh(z + f64(b))

@@ -1,0 +1,52 @@
+import concourse.mybir as mybir
+
+BF16, F32, U16 = mybir.dt.bfloat16, mybir.dt.float32, mybir.dt.uint16
+GELU_TANH = mybir.ActivationFunctionType.Gelu_apprx_tanh
+
+P = 128
+S, M, N, E = 512, 512, 384, 4
+Q = N // E
+QC = Q // 16
+B = M // P
+FLOPS = 2 * P * M * S + 2 * P * M * N
+
+
+def tile_rows_fillproj_gelu_kernel(tc, x, wd, y, w, b, offs, out):
+    nc = tc.nc
+    with (
+        tc.tile_pool(name="held", bufs=1) as held,
+        tc.psum_pool(name="psum", bufs=1) as psum,
+    ):
+        x_tile = held.tile([P, S], BF16, name="x_tile")
+        wd_tile = held.tile([P, M], BF16, name="wd_tile")
+        offsets = held.tile([P, N // 16], U16, name="offsets")
+        y_tile = held.tile([P, N], BF16, name="y_tile")
+        bias = held.tile([P, B], F32, name="bias")
+        experts = [held.tile([P, M], BF16, name=f"expert{e}") for e in range(E)]
+
+        nc.sync.dma_start(x_tile[:], x)
+        nc.sync.dma_start(wd_tile[:], wd)
+        nc.sync.dma_start(offsets[:], offs)
+        nc.sync.dma_start(y_tile[:], y)
+        for e in range(E):
+            nc.sync.dma_start(experts[e][:], w[e])
+        nc.scalar.dma_start(bias[:], b.rearrange("(a p) o -> p (a o)", p=P))
+
+        windows = [psum.tile([P, S], F32, name=f"window{m}") for m in range(B)]
+        for m in range(B):
+            nc.tensor.matmul(windows[m][:], wd_tile[:, m * P : (m + 1) * P], x_tile[:], start=True, stop=False)
+
+        for e in range(E):
+            for m in range(B):
+                nc.tensor.matmul(
+                    windows[m][:].indirect(offsets[:, e * QC : (e + 1) * QC]),
+                    experts[e][:, m * P : (m + 1) * P],
+                    y_tile[:, e * Q : (e + 1) * Q],
+                    start=False,
+                    stop=e == E - 1,
+                )
+
+        for m in range(B):
+            result = held.tile([P, S], F32, name=f"result{m}")
+            nc.scalar.activation(result[:], windows[m][:], GELU_TANH, bias=bias[:, m : m + 1])
+            nc.sync.dma_start(out[m * P : (m + 1) * P, :], result[:])

@@ -8,6 +8,7 @@ S, M, N, E = 512, 512, 384, 4
 Q = N // E
 QC = Q // 16
 B = M // P
+WARM_UPS = 4
 FLOPS = 2 * P * M * S + 2 * P * M * N
 
 
@@ -22,25 +23,35 @@ def tile_rows_fillproj_gelu_kernel(tc, x, wd, y, w, b, offs, out):
         offsets = held.tile([P, N // 16], U16, name="offsets")
         y_tile = held.tile([P, N], BF16, name="y_tile")
         bias = held.tile([P, B], F32, name="bias")
-        experts = [held.tile([P, M], BF16, name=f"expert{e}") for e in range(E)]
+        experts = held.tile([P, E, M], BF16, name="experts")
+        zero = held.tile([P, 1], F32, name="zero")
+        first_gelu = held.tile([P, 1], F32, name="first_gelu")
+        zero_rows = held.tile([P, S], BF16, name="zero_rows")
+        warm_bank = psum.tile([P, S], F32, name="warm_bank")
 
         nc.sync.dma_start(x_tile[:], x)
         nc.sync.dma_start(wd_tile[:], wd)
         nc.sync.dma_start(offsets[:], offs)
         nc.sync.dma_start(y_tile[:], y)
-        for e in range(E):
-            nc.sync.dma_start(experts[e][:], w[e])
+        nc.sync.dma_start(experts[:], w.rearrange("e k m -> k e m"))
         nc.scalar.dma_start(bias[:], b.rearrange("(a p) o -> p (a o)", p=P))
+
+        nc.vector.memset(zero[:], 0.0)
+        nc.scalar.activation(first_gelu[:], zero[:], GELU_TANH, bias=zero[:])
+
+        nc.vector.memset(zero_rows[:], 0.0)
+        for i in range(WARM_UPS):
+            nc.tensor.matmul(warm_bank[:], zero_rows[:, 0:P], zero_rows[:], start=True, stop=True)
 
         windows = [psum.tile([P, S], F32, name=f"window{m}") for m in range(B)]
         for m in range(B):
             nc.tensor.matmul(windows[m][:], wd_tile[:, m * P : (m + 1) * P], x_tile[:], start=True, stop=False)
 
-        for e in range(E):
-            for m in range(B):
+        for m in range(B):
+            for e in range(E):
                 nc.tensor.matmul(
                     windows[m][:].indirect(offsets[:, e * QC : (e + 1) * QC]),
-                    experts[e][:, m * P : (m + 1) * P],
+                    experts[:, e, m * P : (m + 1) * P],
                     y_tile[:, e * Q : (e + 1) * Q],
                     start=False,
                     stop=e == E - 1,

@@ -29,17 +29,18 @@ def tile_rows_fillproj_gelu_kernel(tc, x, wd, y, w, b, offs, out):
         zero_rows = held.tile([P, S], BF16, name="zero_rows")
         warm_bank = psum.tile([P, S], F32, name="warm_bank")
 
+        nc.vector.memset(zero_rows[:], 0.0)
+        nc.vector.memset(zero[:], 0.0)
+
         nc.sync.dma_start(x_tile[:], x)
         nc.sync.dma_start(wd_tile[:], wd)
         nc.sync.dma_start(offsets[:], offs)
         nc.sync.dma_start(y_tile[:], y)
         nc.sync.dma_start(experts[:], w.rearrange("e k m -> k e m"))
-        nc.scalar.dma_start(bias[:], b.rearrange("(a p) o -> p (a o)", p=P))
+        nc.sync.dma_start(bias[:], b.rearrange("(a p) o -> p (a o)", p=P))
 
-        nc.vector.memset(zero[:], 0.0)
         nc.scalar.activation(first_gelu[:], zero[:], GELU_TANH, bias=zero[:])
 
-        nc.vector.memset(zero_rows[:], 0.0)
         for i in range(WARM_UPS):
             nc.tensor.matmul(warm_bank[:], zero_rows[:, 0:P], zero_rows[:], start=True, stop=True)
 

@@ -23,7 +23,7 @@ def tile_rows_fillproj_gelu_kernel(tc, x, wd, y, w, b, offs, out):
         offsets = held.tile([P, N // 16], U16, name="offsets")
         y_tile = held.tile([P, N], BF16, name="y_tile")
         bias = held.tile([P, B], F32, name="bias")
-        experts = held.tile([P, E, M], BF16, name="experts")
+        experts = [held.tile([P, E, M // 2], BF16, name=f"experts{h}") for h in range(2)]
         zero = held.tile([P, 1], F32, name="zero")
         first_gelu = held.tile([P, 1], F32, name="first_gelu")
         zero_rows = held.tile([P, S], BF16, name="zero_rows")
@@ -36,7 +36,9 @@ def tile_rows_fillproj_gelu_kernel(tc, x, wd, y, w, b, offs, out):
         nc.sync.dma_start(wd_tile[:], wd)
         nc.sync.dma_start(offsets[:], offs)
         nc.sync.dma_start(y_tile[:], y)
-        nc.sync.dma_start(experts[:], w.rearrange("e k m -> k e m"))
+        for h in range(2):
+            half = slice(h * M // 2, (h + 1) * M // 2)
+            nc.sync.dma_start(experts[h][:], w[:, :, half].rearrange("e k m -> k e m"))
         nc.sync.dma_start(bias[:], b.rearrange("(a p) o -> p (a o)", p=P))
 
         nc.scalar.activation(first_gelu[:], zero[:], GELU_TANH, bias=zero[:])
@@ -52,13 +54,16 @@ def tile_rows_fillproj_gelu_kernel(tc, x, wd, y, w, b, offs, out):
             for e in range(E):
                 nc.tensor.matmul(
                     windows[m][:].indirect(offsets[:, e * QC : (e + 1) * QC]),
-                    experts[:, e, m * P : (m + 1) * P],
+                    experts[m // 2][:, e, (m % 2) * P : (m % 2 + 1) * P],
                     y_tile[:, e * Q : (e + 1) * Q],
                     start=False,
                     stop=e == E - 1,
                 )
 
         for m in range(B):
-            result = held.tile([P, S], F32, name=f"result{m}")
-            nc.scalar.activation(result[:], windows[m][:], GELU_TANH, bias=bias[:, m : m + 1])
-            nc.sync.dma_start(out[m * P : (m + 1) * P, :], result[:])
+            pieces = 2 if m == B - 1 else 1
+            for i in range(pieces):
+                columns = slice(i * S // pieces, (i + 1) * S // pieces)
+                result = held.tile([P, S // pieces], F32, name=f"result{m}_{i}")
+                nc.scalar.activation(result[:], windows[m][:, columns], GELU_TANH, bias=bias[:, m : m + 1])
+                nc.sync.dma_start(out[m * P : (m + 1) * P, columns], result[:])

@@ -8,7 +8,7 @@ S, M, N, E = 512, 512, 384, 4
 Q = N // E
 QC = Q // 16
 B = M // P
-WARM_UPS = 4
+WARM_UPS, WARM_COLUMNS = 10, 256
 FLOPS = 2 * P * M * S + 2 * P * M * N
 
 
@@ -26,8 +26,8 @@ def tile_rows_fillproj_gelu_kernel(tc, x, wd, y, w, b, offs, out):
         experts = [held.tile([P, E, M // 2], BF16, name=f"experts{h}") for h in range(2)]
         zero = held.tile([P, 1], F32, name="zero")
         first_gelu = held.tile([P, 1], F32, name="first_gelu")
-        zero_rows = held.tile([P, S], BF16, name="zero_rows")
-        warm_bank = psum.tile([P, S], F32, name="warm_bank")
+        zero_rows = held.tile([P, WARM_COLUMNS], BF16, name="zero_rows")
+        warm_bank = psum.tile([P, WARM_COLUMNS], F32, name="warm_bank")
 
         nc.vector.memset(zero_rows[:], 0.0)
         nc.vector.memset(zero[:], 0.0)

import concourse.mybir as mybir

BF16, F32, U16 = mybir.dt.bfloat16, mybir.dt.float32, mybir.dt.uint16
GELU_TANH = mybir.ActivationFunctionType.Gelu_apprx_tanh

P = 128
S, M, N, E = 512, 512, 384, 4
Q = N // E
QC = Q // 16
B = M // P
WARM_UPS, WARM_COLUMNS = 10, 256
FLOPS = 2 * P * M * S + 2 * P * M * N


def tile_rows_fillproj_gelu_kernel(tc, x, wd, y, w, b, offs, out):
    nc = tc.nc
    with (
        tc.tile_pool(name="held", bufs=1) as held,
        tc.psum_pool(name="psum", bufs=1) as psum,
    ):
        x_tile = held.tile([P, S], BF16, name="x_tile")
        wd_tile = held.tile([P, M], BF16, name="wd_tile")
        offsets = held.tile([P, N // 16], U16, name="offsets")
        y_tile = held.tile([P, N], BF16, name="y_tile")
        bias = held.tile([P, B], F32, name="bias")
        experts = [held.tile([P, E, M // 2], BF16, name=f"experts{h}") for h in range(2)]
        zero = held.tile([P, 1], F32, name="zero")
        first_gelu = held.tile([P, 1], F32, name="first_gelu")
        zero_rows = held.tile([P, WARM_COLUMNS], BF16, name="zero_rows")
        warm_bank = psum.tile([P, WARM_COLUMNS], F32, name="warm_bank")

        nc.vector.memset(zero_rows[:], 0.0)
        nc.vector.memset(zero[:], 0.0)

        nc.sync.dma_start(x_tile[:], x)
        nc.sync.dma_start(wd_tile[:], wd)
        nc.sync.dma_start(offsets[:], offs)
        nc.sync.dma_start(y_tile[:], y)
        for h in range(2):
            half = slice(h * M // 2, (h + 1) * M // 2)
            nc.sync.dma_start(experts[h][:], w[:, :, half].rearrange("e k m -> k e m"))
        nc.sync.dma_start(bias[:], b.rearrange("(a p) o -> p (a o)", p=P))

        nc.scalar.activation(first_gelu[:], zero[:], GELU_TANH, bias=zero[:])

        for i in range(WARM_UPS):
            nc.tensor.matmul(warm_bank[:], zero_rows[:, 0:P], zero_rows[:], start=True, stop=True)

        windows = [psum.tile([P, S], F32, name=f"window{m}") for m in range(B)]
        for m in range(B):
            nc.tensor.matmul(windows[m][:], wd_tile[:, m * P : (m + 1) * P], x_tile[:], start=True, stop=False)

        for m in range(B):
            for e in range(E):
                nc.tensor.matmul(
                    windows[m][:].indirect(offsets[:, e * QC : (e + 1) * QC]),
                    experts[m // 2][:, e, (m % 2) * P : (m % 2 + 1) * P],
                    y_tile[:, e * Q : (e + 1) * Q],
                    start=False,
                    stop=e == E - 1,
                )

        for m in range(B):
            pieces = 2 if m == B - 1 else 1
            for i in range(pieces):
                columns = slice(i * S // pieces, (i + 1) * S // pieces)
                result = held.tile([P, S // pieces], F32, name=f"result{m}_{i}")
                nc.scalar.activation(result[:], windows[m][:, columns], GELU_TANH, bias=bias[:, m : m + 1])
                nc.sync.dma_start(out[m * P : (m + 1) * P, columns], result[:])
